import numpy as np
import ml_dtypes


def mxq(x, axis, fmt="e4m3"):
    dtype, down = {"e4m3": (ml_dtypes.float8_e4m3fn, 7), "e5m2": (ml_dtypes.float8_e5m2, 14)}[fmt]
    v = np.moveaxis(np.asarray(x, np.float32).astype(ml_dtypes.bfloat16).astype(np.float64), axis, -1)
    blocks = v.reshape(v.shape[:-1] + (-1, 32))
    amax = np.abs(blocks).max(-1, keepdims=True)
    byte = np.maximum(np.where(amax > 0, np.frexp(amax)[1] - 1 + 127, 0) - down, 1)
    scale = np.exp2(byte - 127.0)
    codes = (blocks / scale).astype(np.float32).astype(dtype).astype(np.float64)
    return np.moveaxis((codes * scale).reshape(v.shape), -1, axis)


WIDE = False


def mx_kscale(k):
    if not WIDE:
        return np.ones(k)
    levels = np.array([10, -10, 5, -5, 0])
    if k % 512:
        return np.exp2(np.random.permutation(np.resize(levels, k // 32))).repeat(32)
    a = np.empty((k // 512, 16))
    for p in range(k // 512):
        a[p, :8] = np.random.permutation(np.resize(levels, 8))
        for g in range(8):
            far = levels[np.abs(levels - a[p, g]) >= 10]
            a[p, g + 8] = far[np.random.randint(len(far))]
    return np.exp2(a.ravel()).repeat(32)


def f64(x):
    return np.asarray(x).astype(np.float64)


def striped(idx):
    return np.tile(idx.reshape(-1, 16).T, (8, 1)).astype(np.uint16)


def unstriped(offs):
    return offs[:16].T.reshape(-1).astype(np.int64)


E2M1 = np.array([0.0, 0.5, 1.0, 1.5, 2.0, 3.0, 4.0, 6.0, -0.0, -0.5, -1.0, -1.5, -2.0, -3.0, -4.0, -6.0])


def pack_weight(w, fmt):
    k, n = w.shape
    w = f64(np.asarray(w, np.float32).astype(ml_dtypes.bfloat16)).reshape(k // 32, 32, n)
    amax = np.abs(w).max(1)
    if fmt == "e4m3":
        byte = np.frexp(amax)[1] - 1 + 127 - 7
    else:
        mant, ex = np.frexp(amax / 6.0)
        byte = np.where(mant > 0.5, ex, ex - 1) + 127
    byte = np.clip(np.where(amax > 0, byte, 1), 1, 254)
    scaled = (w * np.exp2(127.0 - byte)[:, None, :]).reshape(k, n).astype(np.float32)
    by_word = np.ascontiguousarray(scaled.reshape(k // 512, 128, 4, n).transpose(0, 1, 3, 2))
    if fmt == "e4m3":
        words = by_word.astype(ml_dtypes.float8_e4m3fn).view(np.uint8)
    else:
        c = by_word.astype(ml_dtypes.float4_e2m1fn).view(np.uint8) & 0xF
        words = (c[..., 0::2] | (c[..., 1::2] << 4)).reshape(k // 512, 128, 2 * n)
    return np.ascontiguousarray(words), np.ascontiguousarray(byte.astype(np.uint8).reshape(k // 512, 16, n))


def unpack_weight(words, scales, fmt):
    g, _, n = scales.shape
    words = np.ascontiguousarray(words).reshape(g, 128, n, -1)
    if fmt == "e4m3":
        vals = words.view(ml_dtypes.float8_e4m3fn).astype(np.float64)
    else:
        nib = np.empty((g, 128, n, 4), np.uint8)
        nib[..., 0::2] = words & 0xF
        nib[..., 1::2] = words >> 4
        vals = E2M1[nib]
    vals = vals * np.repeat(np.exp2(scales.astype(np.float64) - 127.0), 8, axis=1)[..., None]
    return vals.transpose(0, 1, 3, 2).reshape(g * 512, n)


def gelu(v):
    return 0.5 * v * (1.0 + np.tanh(np.sqrt(2.0 / np.pi) * (v + 0.044715 * v**3)))


K, T, E, C, N = 1024, 4096, 8, 256, 256


def by_expert(wq, xq):
    return np.concatenate([wq[e].T @ xq[:, e * C:(e + 1) * C] for e in range(E)], axis=1)


def setup_inputs():
    n = np.random.standard_normal
    s = mx_kscale(K)[:, None]
    x = pack_weight(n((K, T)) * s, "e4m3")
    return {
        "x_words": x[0],
        "x_scales": x[1],
        "xr": n((N, T)).astype(np.float32),
        "w": (n((E, K, N)) / np.sqrt(K) / s[None]).astype(np.float32),
        "b": (0.3 * n((N, E))).astype(np.float32),
        "gate": np.tile(np.random.uniform(0.2, 1.0, E * C), (N, 1)).astype(np.float32),
        "offs": striped(np.random.permutation(T)[:E * C]),
    }


def reference(x_words, x_scales, xr, w, b, gate, offs):
    idx = unstriped(offs)
    xq = unpack_weight(x_words, x_scales, "e4m3")[:, idx]
    y = by_expert(mxq(f64(w), 1, "e4m3"), xq)
    y = gelu(y + np.repeat(f64(b), C, axis=1))
    out = f64(xr).copy()
    out[:, idx] += f64(gate) * y
    return out

@@ -1,0 +1,179 @@
+from contextlib import ExitStack
+
+import concourse.mybir as mybir
+
+K, T, E, C, N = 1024, 4096, 8, 256, 256
+FLOPS = 2 * K * N * E * C
+BYTES = K * T + K * T // 32 + 4 * (2 * N * T + E * K * N + N * E + E * C) + 2 * 128 * 128
+
+F32 = mybir.dt.float32
+BF16 = mybir.dt.bfloat16
+I32 = mybir.dt.int32
+U32 = mybir.dt.uint32
+U16 = mybir.dt.uint16
+U8 = mybir.dt.uint8
+FP8X4 = mybir.dt.float8_e4m3fn_x4
+GELU = mybir.ActivationFunctionType.Gelu_apprx_tanh
+MULT = mybir.AluOpType.mult
+ADD = mybir.AluOpType.add
+
+P = 128
+PACK = 4
+K_PASS = P * PACK
+PASSES = K // K_PASS
+SLOTS = E * C
+BLOCKS = N // P
+GROUP = 2
+GROUPS = E // GROUP
+WIDTH = GROUP * C
+PIECES = GROUP * PASSES
+STEPS = BLOCKS * GROUPS
+
+
+def tile_moe_res_lin_gelu_kernel(tc, x_words, x_scales, xr, w, b, gate, offs, out):
+    nc = tc.nc
+    with ExitStack() as ctx:
+        lists = ctx.enter_context(tc.tile_pool(name="lists", bufs=1))
+        keep = ctx.enter_context(tc.tile_pool(name="keep", bufs=1))
+        ring = ctx.enter_context(tc.tile_pool(name="ring", bufs=3))
+        psum = ctx.enter_context(tc.psum_pool(name="psum", bufs=3))
+
+        offsets = lists.tile([P, SLOTS // 16], U16, name="offsets")
+        nc.sync.dma_start(offsets[:], offs)
+
+        def entries(first, count):
+            return offsets[:, first // 16 : (first + count) // 16]
+
+        scale_table = keep.tile([P, T], U8, name="scale_table", align_bytes=64)
+        nc.vector.memset(scale_table[:].bitcast(I32), 0)
+        zero = keep.tile([P, 1], F32, name="zero")
+        nc.vector.memset(zero[:], 0.0)
+        windows = [keep.tile([P, T], F32, name=f"window{h}") for h in range(BLOCKS)]
+        for h in range(BLOCKS):
+            nc.scalar.activation(windows[h][:], zero[:].to_broadcast([P, T]), GELU)
+
+        word_tables = [keep.tile([P, T], I32, name=f"word_table{o}") for o in range(PASSES)]
+        slot_words = [keep.tile([P, SLOTS], U32, name=f"slot_words{o}", align_bytes=64) for o in range(PASSES)]
+        slot_scales = keep.tile([P, SLOTS], U8, name="slot_scales", align_bytes=64)
+        raw = {}
+        gates = {}
+        residual = {}
+        acc = {}
+        quantised = {}
+
+        def load_words(o):
+            nc.sync.dma_start(out=word_tables[o][:], in_=x_words[o].rearrange("p t r -> p (t r)").bitcast(I32))
+
+        def gather_words(o, first, count):
+            nc.vector.tensor_copy(
+                slot_words[o][:, first : first + count],
+                word_tables[o][:].bitcast(U32).indirect(entries(first, count)),
+            )
+
+        def load_weights(s):
+            h, g = divmod(s, GROUPS)
+            for i in range(PIECES):
+                a, o = divmod(i, PASSES)
+                raw[s, i] = keep.tile([P, PACK * P], F32, name=f"raw{s}_{i}", tag=f"raw{s}_{i}")
+                rows = w[GROUP * g + a, o * K_PASS : (o + 1) * K_PASS, h * P : (h + 1) * P]
+                nc.sync.dma_start(
+                    out=raw[s, i][:].rearrange("p (j n) -> p j n", j=PACK),
+                    in_=rows.rearrange("(p j) n -> p j n", j=PACK),
+                )
+
+        def load_gate(g):
+            gates[g] = keep.tile([P, WIDTH], F32, name=f"gate{g}")
+            nc.sync.dma_start(out=gates[g][:], in_=gate[0:P, g * WIDTH : (g + 1) * WIDTH])
+
+        def load_residual(h, chunk):
+            for c0 in range(0, T, chunk):
+                residual[h, c0] = keep.tile([P, chunk], F32, name=f"residual{h}_{c0}")
+                nc.sync.dma_start(out=residual[h, c0][:], in_=xr[h * P : (h + 1) * P, c0 : c0 + chunk])
+
+        def quantise(s):
+            grouped = ring.tile([P, PIECES * P * PACK], BF16, name="grouped", align_bytes=64)
+            for i in range(PIECES):
+                part = grouped[:, i * K_PASS : (i + 1) * K_PASS]
+                nc.scalar.copy(
+                    out=part.rearrange("p (c i j) -> p c j i", i=4, j=PACK),
+                    in_=raw[s, i][:].rearrange("p (j c i) -> p c j i", i=4, j=PACK),
+                )
+            codes = ring.tile([P, PIECES * P], U32, name="codes", align_bytes=64)
+            scales = ring.tile([P, PIECES * P], U8, name="scales", align_bytes=64)
+            nc.vector.quantize_mx(out=codes[:].bitcast(FP8X4), scales=scales[:], in_=grouped[:])
+            quantised[s] = (codes, scales)
+
+        def multiply(s):
+            g = s % GROUPS
+            codes, scales = quantised[s]
+            acc[s] = psum.tile([P, WIDTH], F32, name="acc")
+            for a in range(GROUP):
+                cols = slice(g * WIDTH + a * C, g * WIDTH + (a + 1) * C)
+                for o in range(PASSES):
+                    piece = slice((a * PASSES + o) * P, (a * PASSES + o + 1) * P)
+                    nc.tensor.matmul_mx(
+                        out=acc[s][:, a * C : (a + 1) * C],
+                        lhsT=codes[:, piece].bitcast(FP8X4),
+                        lhsT_scale=scales[:, piece],
+                        rhs=slot_words[o][:, cols].bitcast(FP8X4),
+                        rhs_scale=slot_scales[4 * o : P, cols],
+                        start=(o == 0),
+                        stop=(o == PASSES - 1),
+                    )
+
+        def activate_and_scatter(s):
+            h, g = divmod(s, GROUPS)
+            tag = f"raw{s + 1}_{PIECES - 1}" if s + 1 < STEPS else "raw0_0"
+            y = keep.tile([P, WIDTH], F32, name=f"y{s}", tag=tag)
+            for a in range(GROUP):
+                e = GROUP * g + a
+                nc.scalar.activation(
+                    y[:, a * C : (a + 1) * C], acc[s][:, a * C : (a + 1) * C], GELU, bias=bias[:, h, e : e + 1]
+                )
+            nc.vector.tensor_tensor(windows[h][:].indirect(entries(g * WIDTH, WIDTH)), y[:], gates[g][:], MULT)
+
+        def add_and_store(h, chunk):
+            for c0 in range(0, T, chunk):
+                total = residual[h, c0]
+                nc.vector.tensor_tensor(total[:], windows[h][:, c0 : c0 + chunk], total[:], ADD)
+                nc.sync.dma_start(out=out[h * P : (h + 1) * P, c0 : c0 + chunk], in_=total[:])
+
+        load_words(0)
+        for o in range(PASSES):
+            for r in range(4):
+                nc.sync.dma_start(
+                    out=scale_table[4 * o + r : P : 32, :].bitcast(I32),
+                    in_=x_scales[o, r : 16 : 4, :].bitcast(I32),
+                )
+        load_weights(0)
+        load_words(1)
+        bias = keep.tile([P, BLOCKS, E], F32, name="bias")
+        nc.sync.dma_start(out=bias[:], in_=b.rearrange("(h p) e -> p h e", p=P))
+        load_weights(1)
+        load_gate(0)
+        load_weights(2)
+        load_gate(1)
+        load_weights(3)
+        load_gate(2)
+        load_weights(4)
+        load_gate(3)
+        load_weights(5)
+        load_residual(0, 1024)
+        load_weights(6)
+        load_weights(7)
+        load_residual(1, 512)
+
+        gather_words(0, 0, SLOTS)
+        nc.vector.tensor_copy(slot_scales[:], scale_table[:].indirect(offsets[:]))
+        quantise(0)
+        gather_words(1, 0, WIDTH)
+        multiply(0)
+        gather_words(1, WIDTH, SLOTS - WIDTH)
+        for s in range(STEPS):
+            if s + 1 < STEPS:
+                quantise(s + 1)
+                multiply(s + 1)
+            activate_and_scatter(s)
+            if s == GROUPS:
+                add_and_store(0, 1024)
+        add_and_store(1, 512)

@@ -1,6 +1,7 @@
 from contextlib import ExitStack
 
 import concourse.mybir as mybir
+from concourse.masks import make_identity
 
 K, T, E, C, N = 1024, 4096, 8, 256, 256
 FLOPS = 2 * K * N * E * C
@@ -23,11 +24,13 @@ K_PASS = P * PACK
 PASSES = K // K_PASS
 SLOTS = E * C
 BLOCKS = N // P
-GROUP = 2
-GROUPS = E // GROUP
-WIDTH = GROUP * C
-PIECES = GROUP * PASSES
-STEPS = BLOCKS * GROUPS
+PAIR = 2
+PAIRS = E // PAIR
+WIDTH = PAIR * C
+BANK = 512
+SUM_BANKS = 4
+VECTOR_COLUMNS = 1024
+LAST_STORES = [512, 1024, 1024, 1024, 512]
 
 
 def tile_moe_res_lin_gelu_kernel(tc, x_words, x_scales, xr, w, b, gate, offs, out):
@@ -36,7 +39,7 @@ def tile_moe_res_lin_gelu_kernel(tc, x_words, x_scales, xr, w, b, gate, offs, ou
         lists = ctx.enter_context(tc.tile_pool(name="lists", bufs=1))
         keep = ctx.enter_context(tc.tile_pool(name="keep", bufs=1))
         ring = ctx.enter_context(tc.tile_pool(name="ring", bufs=3))
-        psum = ctx.enter_context(tc.psum_pool(name="psum", bufs=3))
+        psum = ctx.enter_context(tc.psum_pool(name="psum", bufs=2))
 
         offsets = lists.tile([P, SLOTS // 16], U16, name="offsets")
         nc.sync.dma_start(offsets[:], offs)
@@ -46,134 +49,172 @@ def tile_moe_res_lin_gelu_kernel(tc, x_words, x_scales, xr, w, b, gate, offs, ou
 
         scale_table = keep.tile([P, T], U8, name="scale_table", align_bytes=64)
         nc.vector.memset(scale_table[:].bitcast(I32), 0)
+        for q in range(4):
+            nc.gpsimd.dma_start(
+                out=scale_table[32 * q : 32 * q + 4 * PASSES, :].bitcast(I32),
+                in_=x_scales[:, 4 * q : 4 * q + 4, :].bitcast(I32),
+            )
         zero = keep.tile([P, 1], F32, name="zero")
         nc.vector.memset(zero[:], 0.0)
         windows = [keep.tile([P, T], F32, name=f"window{h}") for h in range(BLOCKS)]
-        for h in range(BLOCKS):
-            nc.scalar.activation(windows[h][:], zero[:].to_broadcast([P, T]), GELU)
+        nc.scalar.activation(windows[0][:], zero[:].to_broadcast([P, T]), GELU)
+        nc.vector.memset(windows[1][:], 0.0)
+        identity = keep.tile([P, P], F32, name="identity")
+        make_identity(nc, identity[:])
 
-        word_tables = [keep.tile([P, T], I32, name=f"word_table{o}") for o in range(PASSES)]
+        word_tables = [keep.tile([P, T], I32, name=f"word_table{o}", tag=f"word_table{o}") for o in range(PASSES)]
         slot_words = [keep.tile([P, SLOTS], U32, name=f"slot_words{o}", align_bytes=64) for o in range(PASSES)]
-        slot_scales = keep.tile([P, SLOTS], U8, name="slot_scales", align_bytes=64)
+        gates = keep.tile([P, SLOTS], F32, name="gates")
+        slot_scales = {}
         raw = {}
-        gates = {}
-        residual = {}
-        acc = {}
         quantised = {}
+        acc = {}
 
-        def load_words(o):
-            nc.sync.dma_start(out=word_tables[o][:], in_=x_words[o].rearrange("p t r -> p (t r)").bitcast(I32))
-
-        def gather_words(o, first, count):
-            nc.vector.tensor_copy(
-                slot_words[o][:, first : first + count],
-                word_tables[o][:].bitcast(U32).indirect(entries(first, count)),
-            )
-
-        def load_weights(s):
-            h, g = divmod(s, GROUPS)
-            for i in range(PIECES):
-                a, o = divmod(i, PASSES)
-                raw[s, i] = keep.tile([P, PACK * P], F32, name=f"raw{s}_{i}", tag=f"raw{s}_{i}")
-                rows = w[GROUP * g + a, o * K_PASS : (o + 1) * K_PASS, h * P : (h + 1) * P]
-                nc.sync.dma_start(
-                    out=raw[s, i][:].rearrange("p (j n) -> p j n", j=PACK),
-                    in_=rows.rearrange("(p j) n -> p j n", j=PACK),
-                )
-
-        def load_gate(g):
-            gates[g] = keep.tile([P, WIDTH], F32, name=f"gate{g}")
-            nc.sync.dma_start(out=gates[g][:], in_=gate[0:P, g * WIDTH : (g + 1) * WIDTH])
-
-        def load_residual(h, chunk):
-            for c0 in range(0, T, chunk):
-                residual[h, c0] = keep.tile([P, chunk], F32, name=f"residual{h}_{c0}")
-                nc.sync.dma_start(out=residual[h, c0][:], in_=xr[h * P : (h + 1) * P, c0 : c0 + chunk])
-
-        def quantise(s):
-            grouped = ring.tile([P, PIECES * P * PACK], BF16, name="grouped", align_bytes=64)
-            for i in range(PIECES):
-                part = grouped[:, i * K_PASS : (i + 1) * K_PASS]
-                nc.scalar.copy(
-                    out=part.rearrange("p (c i j) -> p c j i", i=4, j=PACK),
-                    in_=raw[s, i][:].rearrange("p (j c i) -> p c j i", i=4, j=PACK),
-                )
-            codes = ring.tile([P, PIECES * P], U32, name="codes", align_bytes=64)
-            scales = ring.tile([P, PIECES * P], U8, name="scales", align_bytes=64)
-            nc.vector.quantize_mx(out=codes[:].bitcast(FP8X4), scales=scales[:], in_=grouped[:])
-            quantised[s] = (codes, scales)
-
-        def multiply(s):
-            g = s % GROUPS
-            codes, scales = quantised[s]
-            acc[s] = psum.tile([P, WIDTH], F32, name="acc")
-            for a in range(GROUP):
-                cols = slice(g * WIDTH + a * C, g * WIDTH + (a + 1) * C)
+        def load_weights(g):
+            for e in range(PAIR * g, PAIR * (g + 1)):
                 for o in range(PASSES):
-                    piece = slice((a * PASSES + o) * P, (a * PASSES + o + 1) * P)
+                    raw[e, o] = keep.tile([P, PACK * N], F32, name=f"raw{e}_{o}", tag=f"raw{e}_{o}")
+                    rows = w[e, o * K_PASS : (o + 1) * K_PASS, :]
+                    nc.sync.dma_start(out=raw[e, o][:], in_=rows.rearrange("(p j) n -> p (j n)", j=PACK))
+
+        def load_columns(tile, rows, first, count):
+            nc.sync.dma_start(out=tile[:, first : first + count], in_=rows[:, first : first + count])
+
+        def gather_scales(first, count, tag):
+            gathered = keep.tile([P, count], U8, name=f"slot_scales{first}", tag=tag, align_bytes=64)
+            nc.vector.tensor_copy(gathered[:], scale_table[:].indirect(entries(first, count)))
+            for c0 in range(first, first + count, C):
+                slot_scales[c0 // C] = (gathered, c0 - first)
+
+        def quantise(g):
+            for e in range(PAIR * g, PAIR * (g + 1)):
+                if e == PAIR - 1:
+                    grouped = keep.tile([P, K * N // P], BF16, name="grouped_once", tag="grouped_once", align_bytes=64)
+                else:
+                    grouped = ring.tile([P, K * N // P], BF16, name="grouped", align_bytes=64)
+                for o in range(PASSES):
+                    part = grouped[:, o * PACK * N : (o + 1) * PACK * N]
+                    nc.scalar.copy(
+                        out=part.rearrange("p (c i j) -> p c j i", i=4, j=PACK),
+                        in_=raw[e, o][:].rearrange("p (j c i) -> p c j i", i=4, j=PACK),
+                    )
+                codes = keep.tile([P, PASSES * N], U32, name=f"codes{e}", align_bytes=64)
+                scales = keep.tile([P, PASSES * N], U8, name=f"scales{e}", align_bytes=64)
+                nc.vector.quantize_mx(out=codes[:].bitcast(FP8X4), scales=scales[:], in_=grouped[:])
+                quantised[e] = (codes, scales)
+
+        def multiply(h, g, bank):
+            acc[h, g] = bank
+            for a in range(PAIR):
+                e = PAIR * g + a
+                codes, scales = quantised[e]
+                token_scales, first = slot_scales[e]
+                for o in range(PASSES):
+                    columns = slice(o * N + h * P, o * N + (h + 1) * P)
                     nc.tensor.matmul_mx(
-                        out=acc[s][:, a * C : (a + 1) * C],
-                        lhsT=codes[:, piece].bitcast(FP8X4),
-                        lhsT_scale=scales[:, piece],
-                        rhs=slot_words[o][:, cols].bitcast(FP8X4),
-                        rhs_scale=slot_scales[4 * o : P, cols],
+                        out=bank[:, a * C : (a + 1) * C],
+                        lhsT=codes[:, columns].bitcast(FP8X4),
+                        lhsT_scale=scales[:, columns],
+                        rhs=slot_words[o][:, e * C : (e + 1) * C].bitcast(FP8X4),
+                        rhs_scale=token_scales[4 * o : P, first : first + C],
                         start=(o == 0),
                         stop=(o == PASSES - 1),
                     )
 
-        def activate_and_scatter(s):
-            h, g = divmod(s, GROUPS)
-            tag = f"raw{s + 1}_{PIECES - 1}" if s + 1 < STEPS else "raw0_0"
-            y = keep.tile([P, WIDTH], F32, name=f"y{s}", tag=tag)
-            for a in range(GROUP):
-                e = GROUP * g + a
+        def activate_and_scatter(h, g, home):
+            y = keep.tile([P, WIDTH], F32, name=f"y{h}_{g}", tag=home)
+            for a in range(PAIR):
+                e = PAIR * g + a
                 nc.scalar.activation(
-                    y[:, a * C : (a + 1) * C], acc[s][:, a * C : (a + 1) * C], GELU, bias=bias[:, h, e : e + 1]
+                    y[:, a * C : (a + 1) * C], acc[h, g][:, a * C : (a + 1) * C], GELU, bias=bias[:, h, e : e + 1]
                 )
-            nc.vector.tensor_tensor(windows[h][:].indirect(entries(g * WIDTH, WIDTH)), y[:], gates[g][:], MULT)
+            slots = slice(g * WIDTH, (g + 1) * WIDTH)
+            nc.vector.tensor_tensor(windows[h][:].indirect(entries(g * WIDTH, WIDTH)), y[:], gates[:, slots], MULT)
 
-        def add_and_store(h, chunk):
-            for c0 in range(0, T, chunk):
-                total = residual[h, c0]
-                nc.vector.tensor_tensor(total[:], windows[h][:, c0 : c0 + chunk], total[:], ADD)
-                nc.sync.dma_start(out=out[h * P : (h + 1) * P, c0 : c0 + chunk], in_=total[:])
+        def add_and_store(h, first, count):
+            total = residual[h][:, first : first + count]
+            nc.vector.tensor_tensor(total, windows[h][:, first : first + count], total, ADD)
+            nc.sync.dma_start(out=out[h * P : (h + 1) * P, first : first + count], in_=total)
 
-        load_words(0)
+        def turn_and_add(c0):
+            sums = psum.tile([P, BANK], F32, name="sums", tag=f"sums{c0 // BANK % SUM_BANKS}", bufs=1)
+            for n, source in enumerate((residual[0], windows[0])):
+                for j in range(0, BANK, P):
+                    nc.tensor.matmul(
+                        sums[:, j : j + P],
+                        lhsT=source[:, c0 + j : c0 + j + P],
+                        rhs=identity[:],
+                        is_transpose=True,
+                        start=(n == 0 and j == 0),
+                        stop=(n == 1 and j == BANK - P),
+                    )
+            turned = ring.tile([P, BANK], F32, name="turned")
+            nc.scalar.copy(turned[:], sums[:])
+            return turned
+
+        def turn_back_and_store(c0, turned):
+            back = psum.tile([P, BANK], F32, name="back")
+            for j in range(0, BANK, P):
+                nc.tensor.transpose(back[:, j : j + P], turned[:, j : j + P], identity[:])
+            total = ring.tile([P, BANK], F32, name="total", bufs=4)
+            nc.scalar.copy(total[:], back[:])
+            nc.scalar.dma_start(out=out[0:P, c0 : c0 + BANK], in_=total[:])
+
         for o in range(PASSES):
-            for r in range(4):
-                nc.sync.dma_start(
-                    out=scale_table[4 * o + r : P : 32, :].bitcast(I32),
-                    in_=x_scales[o, r : 16 : 4, :].bitcast(I32),
-                )
+            nc.sync.dma_start(out=word_tables[o][:], in_=x_words[o].rearrange("p t r -> p (t r)").bitcast(I32))
         load_weights(0)
-        load_words(1)
         bias = keep.tile([P, BLOCKS, E], F32, name="bias")
         nc.sync.dma_start(out=bias[:], in_=b.rearrange("(h p) e -> p h e", p=P))
+        load_columns(gates, gate[0:P, :], 0, SLOTS // 2)
         load_weights(1)
-        load_gate(0)
         load_weights(2)
-        load_gate(1)
+        residual = [keep.tile([P, T], F32, name="residual0")]
+        early = SUM_BANKS * BANK
+        load_columns(residual[0], xr[0:P, :], VECTOR_COLUMNS, early)
         load_weights(3)
-        load_gate(2)
-        load_weights(4)
-        load_gate(3)
-        load_weights(5)
-        load_residual(0, 1024)
-        load_weights(6)
-        load_weights(7)
-        load_residual(1, 512)
+        load_columns(gates, gate[0:P, :], SLOTS // 2, SLOTS // 2)
+        load_columns(residual[0], xr[0:P, :], 0, VECTOR_COLUMNS)
+        load_columns(residual[0], xr[0:P, :], VECTOR_COLUMNS + early, T - VECTOR_COLUMNS - early)
 
-        gather_words(0, 0, SLOTS)
-        nc.vector.tensor_copy(slot_scales[:], scale_table[:].indirect(offsets[:]))
+        for o in range(PASSES):
+            nc.vector.tensor_copy(slot_words[o][:], word_tables[o][:].bitcast(U32).indirect(offsets[:]))
+        residual.append(keep.tile([P, T], F32, name="residual1", tag="word_table0"))
+        for first in range(0, T, 2048):
+            load_columns(residual[1], xr[P:N, :], first, 2048)
+
+        gather_scales(0, WIDTH, "first_scales")
         quantise(0)
-        gather_words(1, 0, WIDTH)
-        multiply(0)
-        gather_words(1, WIDTH, SLOTS - WIDTH)
-        for s in range(STEPS):
-            if s + 1 < STEPS:
-                quantise(s + 1)
-                multiply(s + 1)
-            activate_and_scatter(s)
-            if s == GROUPS:
-                add_and_store(0, 1024)
-        add_and_store(1, 512)
+        multiply(0, 0, psum.tile([P, WIDTH], F32, name="acc", tag="acc_a", bufs=1))
+        gather_scales(WIDTH, SLOTS - WIDTH, "grouped_once")
+        multiply(1, 0, psum.tile([P, WIDTH], F32, name="acc", tag="acc_b", bufs=1))
+        activate_and_scatter(0, 0, "raw0_0")
+        quantise(1)
+        multiply(0, 1, psum.tile([P, WIDTH], F32, name="acc", tag="acc_a", bufs=1))
+        activate_and_scatter(1, 0, "raw3_1")
+        quantise(2)
+        multiply(0, 2, psum.tile([P, WIDTH], F32, name="acc", tag="acc_b", bufs=1))
+        activate_and_scatter(0, 1, "raw5_1")
+        quantise(3)
+        multiply(0, 3, psum.tile([P, WIDTH], F32, name="acc", tag="acc_a", bufs=1))
+        activate_and_scatter(0, 2, "raw7_1")
+        multiply(1, 1, psum.tile([P, WIDTH], F32, name="acc", tag="acc_a", bufs=1))
+        activate_and_scatter(0, 3, "raw0_1")
+        add_and_store(0, 0, VECTOR_COLUMNS)
+        multiply(1, 2, psum.tile([P, WIDTH], F32, name="acc", tag="acc_a", bufs=1))
+        activate_and_scatter(1, 1, "raw1_0")
+        activate_and_scatter(1, 2, "raw1_1")
+
+        waiting = turn_and_add(VECTOR_COLUMNS)
+        for c0 in range(VECTOR_COLUMNS, T, BANK):
+            turned = waiting
+            if c0 + BANK < T:
+                waiting = turn_and_add(c0 + BANK)
+            turn_back_and_store(c0, turned)
+            if c0 == VECTOR_COLUMNS + BANK:
+                tag = f"sums{(c0 + BANK) // BANK % SUM_BANKS}"
+                multiply(1, 3, psum.tile([P, WIDTH], F32, name="last_acc", tag=tag, bufs=1))
+                activate_and_scatter(1, 3, "raw2_0")
+        first = 0
+        for count in LAST_STORES:
+            add_and_store(1, first, count)
+            first = first + count

from contextlib import ExitStack

import concourse.mybir as mybir
from concourse.masks import make_identity

K, T, E, C, N = 1024, 4096, 8, 256, 256
FLOPS = 2 * K * N * E * C
BYTES = K * T + K * T // 32 + 4 * (2 * N * T + E * K * N + N * E + E * C) + 2 * 128 * 128

F32 = mybir.dt.float32
BF16 = mybir.dt.bfloat16
I32 = mybir.dt.int32
U32 = mybir.dt.uint32
U16 = mybir.dt.uint16
U8 = mybir.dt.uint8
FP8X4 = mybir.dt.float8_e4m3fn_x4
GELU = mybir.ActivationFunctionType.Gelu_apprx_tanh
MULT = mybir.AluOpType.mult
ADD = mybir.AluOpType.add

P = 128
PACK = 4
K_PASS = P * PACK
PASSES = K // K_PASS
SLOTS = E * C
BLOCKS = N // P
PAIR = 2
PAIRS = E // PAIR
WIDTH = PAIR * C
BANK = 512
SUM_BANKS = 4
VECTOR_COLUMNS = 1024
LAST_STORES = [512, 1024, 1024, 1024, 512]


def tile_moe_res_lin_gelu_kernel(tc, x_words, x_scales, xr, w, b, gate, offs, out):
    nc = tc.nc
    with ExitStack() as ctx:
        lists = ctx.enter_context(tc.tile_pool(name="lists", bufs=1))
        keep = ctx.enter_context(tc.tile_pool(name="keep", bufs=1))
        ring = ctx.enter_context(tc.tile_pool(name="ring", bufs=3))
        psum = ctx.enter_context(tc.psum_pool(name="psum", bufs=2))

        offsets = lists.tile([P, SLOTS // 16], U16, name="offsets")
        nc.sync.dma_start(offsets[:], offs)

        def entries(first, count):
            return offsets[:, first // 16 : (first + count) // 16]

        scale_table = keep.tile([P, T], U8, name="scale_table", align_bytes=64)
        nc.vector.memset(scale_table[:].bitcast(I32), 0)
        for q in range(4):
            nc.gpsimd.dma_start(
                out=scale_table[32 * q : 32 * q + 4 * PASSES, :].bitcast(I32),
                in_=x_scales[:, 4 * q : 4 * q + 4, :].bitcast(I32),
            )
        zero = keep.tile([P, 1], F32, name="zero")
        nc.vector.memset(zero[:], 0.0)
        windows = [keep.tile([P, T], F32, name=f"window{h}") for h in range(BLOCKS)]
        nc.scalar.activation(windows[0][:], zero[:].to_broadcast([P, T]), GELU)
        nc.vector.memset(windows[1][:], 0.0)
        identity = keep.tile([P, P], F32, name="identity")
        make_identity(nc, identity[:])

        word_tables = [keep.tile([P, T], I32, name=f"word_table{o}", tag=f"word_table{o}") for o in range(PASSES)]
        slot_words = [keep.tile([P, SLOTS], U32, name=f"slot_words{o}", align_bytes=64) for o in range(PASSES)]
        gates = keep.tile([P, SLOTS], F32, name="gates")
        slot_scales = {}
        raw = {}
        quantised = {}
        acc = {}

        def load_weights(g):
            for e in range(PAIR * g, PAIR * (g + 1)):
                for o in range(PASSES):
                    raw[e, o] = keep.tile([P, PACK * N], F32, name=f"raw{e}_{o}", tag=f"raw{e}_{o}")
                    rows = w[e, o * K_PASS : (o + 1) * K_PASS, :]
                    nc.sync.dma_start(out=raw[e, o][:], in_=rows.rearrange("(p j) n -> p (j n)", j=PACK))

        def load_columns(tile, rows, first, count):
            nc.sync.dma_start(out=tile[:, first : first + count], in_=rows[:, first : first + count])

        def gather_scales(first, count, tag):
            gathered = keep.tile([P, count], U8, name=f"slot_scales{first}", tag=tag, align_bytes=64)
            nc.vector.tensor_copy(gathered[:], scale_table[:].indirect(entries(first, count)))
            for c0 in range(first, first + count, C):
                slot_scales[c0 // C] = (gathered, c0 - first)

        def quantise(g):
            for e in range(PAIR * g, PAIR * (g + 1)):
                if e == PAIR - 1:
                    grouped = keep.tile([P, K * N // P], BF16, name="grouped_once", tag="grouped_once", align_bytes=64)
                else:
                    grouped = ring.tile([P, K * N // P], BF16, name="grouped", align_bytes=64)
                for o in range(PASSES):
                    part = grouped[:, o * PACK * N : (o + 1) * PACK * N]
                    nc.scalar.copy(
                        out=part.rearrange("p (c i j) -> p c j i", i=4, j=PACK),
                        in_=raw[e, o][:].rearrange("p (j c i) -> p c j i", i=4, j=PACK),
                    )
                codes = keep.tile([P, PASSES * N], U32, name=f"codes{e}", align_bytes=64)
                scales = keep.tile([P, PASSES * N], U8, name=f"scales{e}", align_bytes=64)
                nc.vector.quantize_mx(out=codes[:].bitcast(FP8X4), scales=scales[:], in_=grouped[:])
                quantised[e] = (codes, scales)

        def multiply(h, g, bank):
            acc[h, g] = bank
            for a in range(PAIR):
                e = PAIR * g + a
                codes, scales = quantised[e]
                token_scales, first = slot_scales[e]
                for o in range(PASSES):
                    columns = slice(o * N + h * P, o * N + (h + 1) * P)
                    nc.tensor.matmul_mx(
                        out=bank[:, a * C : (a + 1) * C],
                        lhsT=codes[:, columns].bitcast(FP8X4),
                        lhsT_scale=scales[:, columns],
                        rhs=slot_words[o][:, e * C : (e + 1) * C].bitcast(FP8X4),
                        rhs_scale=token_scales[4 * o : P, first : first + C],
                        start=(o == 0),
                        stop=(o == PASSES - 1),
                    )

        def activate_and_scatter(h, g, home):
            y = keep.tile([P, WIDTH], F32, name=f"y{h}_{g}", tag=home)
            for a in range(PAIR):
                e = PAIR * g + a
                nc.scalar.activation(
                    y[:, a * C : (a + 1) * C], acc[h, g][:, a * C : (a + 1) * C], GELU, bias=bias[:, h, e : e + 1]
                )
            slots = slice(g * WIDTH, (g + 1) * WIDTH)
            nc.vector.tensor_tensor(windows[h][:].indirect(entries(g * WIDTH, WIDTH)), y[:], gates[:, slots], MULT)

        def add_and_store(h, first, count):
            total = residual[h][:, first : first + count]
            nc.vector.tensor_tensor(total, windows[h][:, first : first + count], total, ADD)
            nc.sync.dma_start(out=out[h * P : (h + 1) * P, first : first + count], in_=total)

        def turn_and_add(c0):
            sums = psum.tile([P, BANK], F32, name="sums", tag=f"sums{c0 // BANK % SUM_BANKS}", bufs=1)
            for n, source in enumerate((residual[0], windows[0])):
                for j in range(0, BANK, P):
                    nc.tensor.matmul(
                        sums[:, j : j + P],
                        lhsT=source[:, c0 + j : c0 + j + P],
                        rhs=identity[:],
                        is_transpose=True,
                        start=(n == 0 and j == 0),
                        stop=(n == 1 and j == BANK - P),
                    )
            turned = ring.tile([P, BANK], F32, name="turned")
            nc.scalar.copy(turned[:], sums[:])
            return turned

        def turn_back_and_store(c0, turned):
            back = psum.tile([P, BANK], F32, name="back")
            for j in range(0, BANK, P):
                nc.tensor.transpose(back[:, j : j + P], turned[:, j : j + P], identity[:])
            total = ring.tile([P, BANK], F32, name="total", bufs=4)
            nc.scalar.copy(total[:], back[:])
            nc.scalar.dma_start(out=out[0:P, c0 : c0 + BANK], in_=total[:])

        for o in range(PASSES):
            nc.sync.dma_start(out=word_tables[o][:], in_=x_words[o].rearrange("p t r -> p (t r)").bitcast(I32))
        load_weights(0)
        bias = keep.tile([P, BLOCKS, E], F32, name="bias")
        nc.sync.dma_start(out=bias[:], in_=b.rearrange("(h p) e -> p h e", p=P))
        load_columns(gates, gate[0:P, :], 0, SLOTS // 2)
        load_weights(1)
        load_weights(2)
        residual = [keep.tile([P, T], F32, name="residual0")]
        early = SUM_BANKS * BANK
        load_columns(residual[0], xr[0:P, :], VECTOR_COLUMNS, early)
        load_weights(3)
        load_columns(gates, gate[0:P, :], SLOTS // 2, SLOTS // 2)
        load_columns(residual[0], xr[0:P, :], 0, VECTOR_COLUMNS)
        load_columns(residual[0], xr[0:P, :], VECTOR_COLUMNS + early, T - VECTOR_COLUMNS - early)

        for o in range(PASSES):
            nc.vector.tensor_copy(slot_words[o][:], word_tables[o][:].bitcast(U32).indirect(offsets[:]))
        residual.append(keep.tile([P, T], F32, name="residual1", tag="word_table0"))
        for first in range(0, T, 2048):
            load_columns(residual[1], xr[P:N, :], first, 2048)

        gather_scales(0, WIDTH, "first_scales")
        quantise(0)
        multiply(0, 0, psum.tile([P, WIDTH], F32, name="acc", tag="acc_a", bufs=1))
        gather_scales(WIDTH, SLOTS - WIDTH, "grouped_once")
        multiply(1, 0, psum.tile([P, WIDTH], F32, name="acc", tag="acc_b", bufs=1))
        activate_and_scatter(0, 0, "raw0_0")
        quantise(1)
        multiply(0, 1, psum.tile([P, WIDTH], F32, name="acc", tag="acc_a", bufs=1))
        activate_and_scatter(1, 0, "raw3_1")
        quantise(2)
        multiply(0, 2, psum.tile([P, WIDTH], F32, name="acc", tag="acc_b", bufs=1))
        activate_and_scatter(0, 1, "raw5_1")
        quantise(3)
        multiply(0, 3, psum.tile([P, WIDTH], F32, name="acc", tag="acc_a", bufs=1))
        activate_and_scatter(0, 2, "raw7_1")
        multiply(1, 1, psum.tile([P, WIDTH], F32, name="acc", tag="acc_a", bufs=1))
        activate_and_scatter(0, 3, "raw0_1")
        add_and_store(0, 0, VECTOR_COLUMNS)
        multiply(1, 2, psum.tile([P, WIDTH], F32, name="acc", tag="acc_a", bufs=1))
        activate_and_scatter(1, 1, "raw1_0")
        activate_and_scatter(1, 2, "raw1_1")

        waiting = turn_and_add(VECTOR_COLUMNS)
        for c0 in range(VECTOR_COLUMNS, T, BANK):
            turned = waiting
            if c0 + BANK < T:
                waiting = turn_and_add(c0 + BANK)
            turn_back_and_store(c0, turned)
            if c0 == VECTOR_COLUMNS + BANK:
                tag = f"sums{(c0 + BANK) // BANK % SUM_BANKS}"
                multiply(1, 3, psum.tile([P, WIDTH], F32, name="last_acc", tag=tag, bufs=1))
                activate_and_scatter(1, 3, "raw2_0")
        first = 0
        for count in LAST_STORES:
            add_and_store(1, first, count)
            first = first + count
